import numpy as np
import ml_dtypes


def mxq(x, axis, fmt="e4m3"):
    dtype, down = {"e4m3": (ml_dtypes.float8_e4m3fn, 7), "e5m2": (ml_dtypes.float8_e5m2, 14)}[fmt]
    v = np.moveaxis(np.asarray(x, np.float32).astype(ml_dtypes.bfloat16).astype(np.float64), axis, -1)
    blocks = v.reshape(v.shape[:-1] + (-1, 32))
    amax = np.abs(blocks).max(-1, keepdims=True)
    byte = np.maximum(np.where(amax > 0, np.frexp(amax)[1] - 1 + 127, 0) - down, 1)
    scale = np.exp2(byte - 127.0)
    codes = (blocks / scale).astype(np.float32).astype(dtype).astype(np.float64)
    return np.moveaxis((codes * scale).reshape(v.shape), -1, axis)


WIDE = False


def mx_kscale(k):
    if not WIDE:
        return np.ones(k)
    levels = np.array([10, -10, 5, -5, 0])
    if k % 512:
        return np.exp2(np.random.permutation(np.resize(levels, k // 32))).repeat(32)
    a = np.empty((k // 512, 16))
    for p in range(k // 512):
        a[p, :8] = np.random.permutation(np.resize(levels, 8))
        for g in range(8):
            far = levels[np.abs(levels - a[p, g]) >= 10]
            a[p, g + 8] = far[np.random.randint(len(far))]
    return np.exp2(a.ravel()).repeat(32)


def f64(x):
    return np.asarray(x).astype(np.float64)


def striped(idx):
    return np.tile(idx.reshape(-1, 16).T, (8, 1)).astype(np.uint16)


def unstriped(offs):
    return offs[:16].T.reshape(-1).astype(np.int64)


def pack_weight(w):
    k, n = w.shape
    w = f64(np.asarray(w, np.float32).astype(ml_dtypes.bfloat16)).reshape(k // 32, 32, n)
    amax = np.abs(w).max(1)
    byte = np.clip(np.where(amax > 0, np.frexp(amax)[1] - 1 + 127 - 7, 1), 1, 254)
    scaled = (w * np.exp2(127.0 - byte)[:, None, :]).reshape(k, n).astype(np.float32)
    words = np.ascontiguousarray(scaled.reshape(k // 512, 128, 4, n).transpose(0, 1, 3, 2)).astype(ml_dtypes.float8_e4m3fn).view(np.uint8)
    return words, np.ascontiguousarray(byte.astype(np.uint8).reshape(k // 512, 16, n))


def unpack_weight(words, scales):
    g, p, n, _ = words.shape
    vals = np.ascontiguousarray(words).view(ml_dtypes.float8_e4m3fn).astype(np.float64) * np.repeat(np.exp2(scales.astype(np.float64) - 127.0), 8, axis=1)[..., None]
    return vals.transpose(0, 1, 3, 2).reshape(g * 512, n)


E2M1 = np.array([0.0, 0.5, 1.0, 1.5, 2.0, 3.0, 4.0, 6.0, -0.0, -0.5, -1.0, -1.5, -2.0, -3.0, -4.0, -6.0])


def pack_fp4(w):
    k, n = w.shape
    w = f64(np.asarray(w, np.float32).astype(ml_dtypes.bfloat16)).reshape(k // 32, 32, n)
    amax = np.abs(w).max(1)
    mant, ex = np.frexp(amax / 6.0)
    byte = np.clip(np.where(amax > 0, np.where(mant > 0.5, ex, ex - 1) + 127, 1), 1, 254)
    scaled = (w * np.exp2(127.0 - byte)[:, None, :]).reshape(k, n).astype(np.float32)
    c = np.ascontiguousarray(scaled.reshape(k // 512, 128, 4, n).transpose(0, 1, 3, 2)).astype(ml_dtypes.float4_e2m1fn).view(np.uint8) & 0xF
    words = (c[..., 0::2] | (c[..., 1::2] << 4)).reshape(k // 512, 128, 2 * n)
    return np.ascontiguousarray(words), np.ascontiguousarray(byte.astype(np.uint8).reshape(k // 512, 16, n))


def unpack_fp4(words, scales):
    g, _, n = scales.shape
    words = np.ascontiguousarray(words).reshape(g, 128, n, 2)
    nib = np.empty((g, 128, n, 4), np.uint8)
    nib[..., 0::2] = words & 0xF
    nib[..., 1::2] = words >> 4
    vals = E2M1[nib] * np.repeat(np.exp2(scales.astype(np.float64) - 127.0), 8, axis=1)[..., None]
    return vals.transpose(0, 1, 3, 2).reshape(g * 512, n)


def sigmoid(v):
    return 1.0 / (1.0 + np.exp(-np.maximum(v, -700.0)))


K, T, S, D, N, H, V, U = 1024, 2048, 1024, 4, 256, 512, 256, 512


def setup_inputs():
    n = np.random.standard_normal
    s = mx_kscale(K)[:, None]
    u = mx_kscale(H)
    packed_xT = pack_weight(n((K, T)) * s)
    packed_w1 = pack_fp4(n((K, H)) / np.sqrt(K) / s)
    packed_w2 = pack_fp4(n((K, H)) / np.sqrt(K) / s)
    packed_w3 = pack_fp4(n((H, N)) / np.sqrt(H) / u[:, None])
    return {
        "x_words": packed_xT[0],
        "x_scales": packed_xT[1],
        "w1_words": packed_w1[0],
        "w1_scales": packed_w1[1],
        "w2_words": packed_w2[0],
        "w2_scales": packed_w2[1],
        "unit": (np.random.uniform(0.6, 1.4, (H, 1)) * u[:, None]).astype(np.float32),
        "w3_words": packed_w3[0],
        "w3_scales": packed_w3[1],
        "offs": striped(np.random.permutation(T)[:S]),
        "pix": striped(np.random.permutation(np.concatenate([np.arange(V), np.random.randint(0, V, U - V)]))),
    }


def reference(x_words, x_scales, w1_words, w1_scales, w2_words, w2_scales, unit, w3_words, w3_scales, offs, pix):
    xq = unpack_weight(x_words, x_scales)[:, unstriped(offs)]
    sd = unpack_fp4(w1_words, w1_scales).T @ xq
    cdf = sigmoid(2.5 * sd)
    alf = np.maximum((cdf - (np.pad(cdf, ((0, 0), (0, 1)))[:, 1:])) / (cdf + 0.1), 0.1 * cdf)
    tr = -1.0 * alf + 1.0
    we = alf * (np.pad(tr, ((0, 0), (1, 0)))[:, :S])
    ft = unpack_fp4(w2_words, w2_scales).T @ xq
    wf = we * ft
    ray = wf.reshape(len(wf), -1, D).sum(axis=2)
    cp = ray[:, unstriped(pix)]
    hit = alf.reshape(len(alf), -1, D).max(axis=2)
    hid = f64(unit) * (cp * hit[:, unstriped(pix)])
    return unpack_fp4(w3_words, w3_scales).T @ mxq(hid, 0, "e4m3")

@@ -1,0 +1,245 @@
+import math
+from contextlib import ExitStack
+
+import concourse.mybir as mybir
+from concourse.masks import make_identity
+
+K, T, S, D, N, H, V, U = 1024, 2048, 1024, 4, 256, 512, 256, 512
+FLOPS = 2 * (2 * K * H * S + H * N * U)
+
+F32 = mybir.dt.float32
+BF16 = mybir.dt.bfloat16
+I32 = mybir.dt.int32
+U32 = mybir.dt.uint32
+U16 = mybir.dt.uint16
+U8 = mybir.dt.uint8
+FP8X4 = mybir.dt.float8_e4m3fn_x4
+FP4X4 = mybir.dt.float4_e2m1fn_x4
+ALU = mybir.AluOpType
+ACT = mybir.ActivationFunctionType
+
+P = 128
+PACK = 4
+PASSES = K // (P * PACK)
+BANK = 512
+HALVES = S // BANK
+PIX_HALF = U // 2
+LEAD = 8
+RATIO = 100.0 / 11.0
+
+
+def tile_picked_yneusa_hit_p_kernel(
+    tc, x_words, x_scales, w1_words, w1_scales, w2_words, w2_scales, unit, w3_words, w3_scales, offs, pix, out
+):
+    nc = tc.nc
+    with ExitStack() as ctx:
+        keep = ctx.enter_context(tc.tile_pool(name="keep", bufs=1))
+        ring = ctx.enter_context(tc.tile_pool(name="ring", bufs=2))
+        psum = ctx.enter_context(tc.psum_pool(name="psum", bufs=1))
+
+        offs_sb = keep.tile([P, S // 16], U16, name="offs_sb")
+        pix_sb = keep.tile([P, U // 16], U16, name="pix_sb")
+        nc.sync.dma_start(offs_sb[:], offs)
+
+        xs_win = keep.tile([P, T], U8, name="xs_win", align_bytes=64)
+        ws_raw = keep.tile([P, PASSES, H], U8, name="ws_raw", align_bytes=64)
+        ww_raw = keep.tile([P, PASSES, 2 * H], U8, name="ww_raw", align_bytes=64)
+        xs_second = keep.tile([P, S], U8, name="xs_second", align_bytes=64)
+        nc.vector.memset(xs_win[:].bitcast(I32), 0)
+        nc.gpsimd.memset(ws_raw[:].bitcast(I32), 0)
+        nc.gpsimd.memset(xs_second[:].bitcast(I32), 0)
+        for q in range(4):
+            nc.sync.dma_start(xs_win[32 * q : 32 * q + 8, :].bitcast(I32), x_scales[:, 4 * q : 4 * q + 4, :].bitcast(I32))
+
+        def load_weight(words, scales):
+            nc.sync.dma_start(ww_raw[:].bitcast(I32), words.rearrange("o p n -> p o n").bitcast(I32))
+            for q in range(4):
+                nc.scalar.dma_start(
+                    ws_raw[32 * q : 32 * q + 4, :, :].bitcast(I32),
+                    scales[:, 4 * q : 4 * q + 4, :].rearrange("o r n -> r o n").bitcast(I32),
+                )
+
+        def deal_weight(name):
+            words = keep.tile([P, PACK, PASSES, 2 * P], U8, name=name + "_words", align_bytes=64)
+            scales = keep.tile([P, PACK, PASSES, P], U8, name=name + "_scales", align_bytes=64)
+            nc.vector.tensor_copy(
+                words[:].bitcast(U16).rearrange("p t o m -> p t (o m)").rearrange("p t (g i) -> p g t i", i=8),
+                ww_raw[:].bitcast(U16).rearrange("p o n -> p (o n)").rearrange("p (g i t) -> p g t i", i=8, t=PACK),
+            )
+            nc.vector.tensor_copy(
+                scales[:].rearrange("p t o m -> p t (o m)").rearrange("p t (g i) -> p g t i", i=16),
+                ws_raw[:].rearrange("p o n -> p (o n)").rearrange("p (g i t) -> p g t i", i=16, t=PACK),
+            )
+            return words, scales
+
+        load_weight(w1_words, w1_scales)
+        xw_win = [keep.tile([P, T], U32, name=f"xw_win{o}", align_bytes=64) for o in range(PASSES)]
+        for o in range(PASSES):
+            nc.sync.dma_start(xw_win[o][:].bitcast(I32), x_words[o].rearrange("p n t -> p (n t)").bitcast(I32))
+
+        xs_both = keep.tile([P, S], U8, name="xs_both", align_bytes=64)
+        nc.vector.tensor_copy(xs_both[:], xs_win[:].indirect(offs_sb[:]))
+        nc.sync.dma_start(xs_second[0:100, :].bitcast(I32), xs_both[4:104, :].bitcast(I32))
+        x_planes = [xs_both, xs_second]
+
+        w1_dealt = deal_weight("w1")
+        load_weight(w2_words, w2_scales)
+
+        xg = [[keep.tile([P, BANK], U32, name=f"xg{o}{h}", align_bytes=64) for h in range(HALVES)] for o in range(PASSES)]
+        for o in range(PASSES):
+            for h in range(HALVES):
+                cols = slice(h * BANK // 16, (h + 1) * BANK // 16)
+                nc.vector.tensor_copy(xg[o][h][:], xw_win[o][:].indirect(offs_sb[:, cols]))
+
+        w2_dealt = deal_weight("w2")
+        nc.sync.dma_start(ww_raw[:, 0, 0 : 2 * N].bitcast(I32), w3_words[0].bitcast(I32))
+        for q in range(4):
+            nc.sync.dma_start(ws_raw[32 * q : 32 * q + 4, 0, 0:N].bitcast(I32), w3_scales[0, 4 * q : 4 * q + 4, :].bitcast(I32))
+        nc.sync.dma_start(pix_sb[:], pix)
+        unit_sb = keep.tile([P, PACK], F32, name="unit_sb")
+        nc.gpsimd.dma_start(unit_sb[:], unit.rearrange("(p t) o -> p (t o)", t=PACK))
+        gain = keep.tile([P, PACK], F32, name="gain")
+        nc.gpsimd.tensor_scalar(gain[:], unit_sb[:], -0.001, 0.0, ALU.mult, ALU.add)
+
+        cdf = [keep.tile([P, D, V + LEAD], F32, name=f"cdf{b}") for b in range(2)]
+        alf = [keep.tile([P, D, LEAD + V], F32, name=f"alf{b}") for b in range(2)]
+        for b in range(2):
+            nc.gpsimd.memset(cdf[b][:, 0, V : V + 1], 0.0)
+            nc.gpsimd.memset(alf[b][:, D - 1, LEAD - 1 : LEAD], 10.0)
+        ident = keep.tile([P, P], F32, name="ident")
+        make_identity(nc, ident[:])
+
+        def product(dealt, t, h, tag, bufs):
+            words, scales = dealt
+            acc = psum.tile([P, BANK], F32, name=tag, bufs=bufs)
+            for o in range(PASSES):
+                nc.tensor.matmul_mx(
+                    out=acc[:],
+                    lhsT=words[:, t, o, :].bitcast(FP4X4),
+                    lhsT_scale=scales[:, t, o, :],
+                    rhs=xg[o][h][:].bitcast(FP8X4),
+                    rhs_scale=x_planes[o][:, h * BANK : (h + 1) * BANK],
+                    start=(o == 0),
+                    stop=(o == PASSES - 1),
+                )
+            return acc[:].rearrange("p (v d) -> p d v", d=D)
+
+        picked = [keep.tile([P, PACK, PIX_HALF], BF16, name=f"picked{h}") for h in range(2)]
+        woven = [keep.tile([P, PIX_HALF, PACK], BF16, name=f"woven{h}", align_bytes=64) for h in range(2)]
+        rays = [slice(h * P, (h + 1) * P) for h in range(HALVES)]
+        recip, ratio, we, wf, ft, window, ray = {}, {}, {}, {}, {}, {}, {}
+
+        def shifted(vs, by):
+            return slice(vs.start + by, vs.stop + by)
+
+        def sigmoids(t):
+            far = ring.tile([P, D, V], F32, name="far")
+            recip[t] = ring.tile([P, D, V], F32, name="recip")
+            for h in range(HALVES):
+                sd = product(w1_dealt, t, h, "sd", 4)
+                nc.scalar.activation(cdf[t % 2][:, :, rays[h]], sd, ACT.Sigmoid, scale=2.5)
+                nc.scalar.activation(far[:, :, rays[h]], sd, ACT.Sigmoid, scale=-2.5, bias=-math.log(11.0))
+                if t > 0:
+                    nc.scalar.activation(recip[t][:, :, rays[h]], far[:, :, rays[h]], ACT.Copy, scale=-10.0 * RATIO, bias=-RATIO)
+            ft[t] = [product(w2_dealt, t, h, "ft", 2) for h in range(HALVES)]
+            ratio[t] = ring.tile([P, D, V], F32, name="ratio")
+            we[t] = ring.tile([P, D, V], F32, name="we")
+            wf[t] = ring.tile([P, HALVES, D, P], F32, name="wf")
+            window[t] = ring.tile([P, 2 * V], F32, name="window", bufs=4)
+            return far
+
+        def ratios(t, vs):
+            c = cdf[t % 2]
+            nc.vector.scalar_tensor_tensor(ratio[t][:, : D - 1, vs], c[:, 1:, vs], 0.1, recip[t][:, : D - 1, vs], ALU.add, ALU.mult)
+            nc.vector.scalar_tensor_tensor(ratio[t][:, D - 1, vs], c[:, 0, shifted(vs, 1)], 0.1, recip[t][:, D - 1, vs], ALU.add, ALU.mult)
+
+        def opacities(t, vs):
+            nc.vector.scalar_tensor_tensor(alf[t % 2][:, :, shifted(vs, LEAD)], ratio[t][:, :, vs], 10.0, cdf[t % 2][:, :, vs], ALU.add, ALU.max)
+
+        def weights_and_hits(t):
+            a = alf[t % 2]
+            alf_pairs = ring.tile([P, 2, V], F32, name="alf_pairs")
+            nc.vector.scalar_tensor_tensor(we[t][:, 1:, :], a[:, : D - 1, LEAD:], -10.0, a[:, 1:, LEAD:], ALU.add, ALU.mult)
+            nc.vector.tensor_tensor(alf_pairs[:], a[:, 0:2, LEAD:], a[:, 2:4, LEAD:], ALU.max)
+            nc.vector.scalar_tensor_tensor(we[t][:, 0, :], a[:, D - 1, LEAD - 1 : LEAD - 1 + V], -10.0, a[:, 0, LEAD:], ALU.add, ALU.mult)
+            nc.vector.tensor_tensor(window[t][:, V:], alf_pairs[:, 0, :], alf_pairs[:, 1, :], ALU.max)
+
+        def weighted(t, h):
+            nc.vector.tensor_tensor(wf[t][:, h], ft[t][h], we[t][:, :, rays[h]], ALU.mult)
+
+        def ray_sums_on_tensor(t):
+            turned = psum.tile([P, HALVES, P], F32, name="turned", bufs=1)
+            for h in range(HALVES):
+                for d in range(D):
+                    nc.tensor.matmul(turned[:, h, :], wf[t][:, h, d, :], ident[:], is_transpose=True, start=(d == 0), stop=(d == D - 1))
+            turned_sb = ring.tile([P, HALVES, P], F32, name="turned_sb")
+            nc.scalar.copy(turned_sb[:], turned[:])
+            ray[t] = psum.tile([P, V], F32, name="ray_bank", bufs=1)
+            for h in range(HALVES):
+                nc.tensor.transpose(ray[t][:, rays[h]], turned_sb[:, h, :], ident[:])
+
+        def look_up(t):
+            nc.vector.scalar_tensor_tensor(window[t][:, :V], ray[t][:], gain[:, t : t + 1], window[t][:, V:], ALU.mult, ALU.mult)
+            for h in range(2):
+                looked_up = window[t][:].indirect(pix_sb[:, h * PIX_HALF // 16 : (h + 1) * PIX_HALF // 16])
+                if t == PACK - 1 and h == 0:
+                    nc.vector.tensor_copy(picked[h][:, t, :], looked_up)
+                else:
+                    nc.scalar.activation(picked[h][:, t, :], looked_up, ACT.Copy)
+            if t == 1:
+                for h in range(2):
+                    nc.scalar.copy(woven[h][:, :, 0:2], picked[h][:, 0:2, :].rearrange("p t r -> p r t"))
+
+        for t in range(PACK):
+            far = sigmoids(t)
+            if t == 0:
+                for h in range(HALVES):
+                    nc.vector.tensor_scalar(recip[t][:, :, rays[h]], far[:, :, rays[h]], -10.0 * RATIO, -RATIO, ALU.mult, ALU.add)
+                for h in range(HALVES):
+                    ratios(t, rays[h])
+                for h in range(HALVES):
+                    opacities(t, rays[h])
+            else:
+                ratios(t, slice(0, V))
+                weighted(t - 1, 0)
+                opacities(t, slice(0, V))
+                weighted(t - 1, 1)
+                ray_sums_on_tensor(t - 1)
+            weights_and_hits(t)
+            if 0 < t < PACK - 1:
+                look_up(t - 1)
+        last = PACK - 1
+        weighted(last, 0)
+        weighted(last, 1)
+        look_up(last - 1)
+        wf_pairs = keep.tile([P, HALVES, 2, P], F32, name="wf_pairs")
+        nc.vector.tensor_tensor(wf_pairs[:], wf[last][:, :, 0:2, :], wf[last][:, :, 2:4, :], ALU.add)
+        ray[last] = keep.tile([P, V], F32, name="ray_last")
+        nc.vector.tensor_tensor(ray[last][:].rearrange("p (h v) -> p h v", h=HALVES), wf_pairs[:, :, 0, :], wf_pairs[:, :, 1, :], ALU.add)
+        look_up(last)
+
+        out_view = out.rearrange("(m p) r -> p m r", p=P)
+        codes = [keep.tile([P, PIX_HALF], U32, name=f"codes{h}", align_bytes=64) for h in range(2)]
+        planes = [keep.tile([P, PIX_HALF], U8, name=f"planes{h}", align_bytes=64) for h in range(2)]
+        nc.vector.tensor_copy(woven[0][:, :, 2:4], picked[0][:, 2:4, :].rearrange("p t r -> p r t"))
+        nc.scalar.copy(woven[1][:, :, 2:4], picked[1][:, 2:4, :].rearrange("p t r -> p r t"))
+        for h in range(2):
+            nc.vector.quantize_mx(out=codes[h][:].bitcast(FP8X4), scales=planes[h][:], in_=woven[h][:].rearrange("p r t -> p (r t)"))
+            acc = psum.tile([P, BANK], F32, name="sd", bufs=4)
+            for m in range(N // P):
+                nc.tensor.matmul_mx(
+                    out=acc[:, m * PIX_HALF : (m + 1) * PIX_HALF],
+                    lhsT=ww_raw[:, 0, 2 * P * m : 2 * P * (m + 1)].bitcast(FP4X4),
+                    lhsT_scale=ws_raw[:, 0, P * m : P * (m + 1)],
+                    rhs=codes[h][:].bitcast(FP8X4),
+                    rhs_scale=planes[h][:],
+                    start=True,
+                    stop=True,
+                )
+            result = keep.tile([P, N // P, PIX_HALF], F32, name=f"result{h}")
+            if h == 0:
+                nc.scalar.copy(result[:].rearrange("p m r -> p (m r)"), acc[:])
+                nc.scalar.dma_start(out_view[:, :, 0:PIX_HALF], result[:])
+            else:
+                nc.vector.tensor_copy(result[:].rearrange("p m r -> p (m r)"), acc[:])
+                nc.sync.dma_start(out_view[:, :, PIX_HALF:], result[:])

@@ -41,60 +41,80 @@ def tile_picked_yneusa_hit_p_kernel(
         pix_sb = keep.tile([P, U // 16], U16, name="pix_sb")
         nc.sync.dma_start(offs_sb[:], offs)
 
-        xs_win = keep.tile([P, T], U8, name="xs_win", align_bytes=64)
-        ws_raw = keep.tile([P, PASSES, H], U8, name="ws_raw", align_bytes=64)
+        xs_win = keep.tile([P, T], U8, name="xs_win", tag="xs_win", align_bytes=64)
+        ws_raw = [keep.tile([P, PASSES, H], U8, name=f"ws_raw{w}", align_bytes=64) for w in range(2)]
         ww_raw = keep.tile([P, PASSES, 2 * H], U8, name="ww_raw", align_bytes=64)
-        xs_second = keep.tile([P, S], U8, name="xs_second", align_bytes=64)
-        nc.vector.memset(xs_win[:].bitcast(I32), 0)
-        nc.gpsimd.memset(ws_raw[:].bitcast(I32), 0)
-        nc.gpsimd.memset(xs_second[:].bitcast(I32), 0)
+        x_planes = [keep.tile([P, S], U8, name=f"x_plane{o}", align_bytes=64) for o in range(PASSES)]
         for q in range(4):
-            nc.sync.dma_start(xs_win[32 * q : 32 * q + 8, :].bitcast(I32), x_scales[:, 4 * q : 4 * q + 4, :].bitcast(I32))
+            nc.sync.dma_start(xs_win[32 * q + 24 : 32 * q + 32, :].bitcast(I32), x_scales[:, 4 * q : 4 * q + 4, :].bitcast(I32))
+        for w in range(2):
+            nc.gpsimd.memset(ws_raw[w][:].bitcast(I32), 0)
+        for q in range(4):
+            (nc.vector if q % 2 else nc.gpsimd).memset(xs_win[32 * q : 32 * q + 24, :].bitcast(I32), 0)
+        for o in range(PASSES):
+            nc.gpsimd.memset(x_planes[o][96:128, :].bitcast(I32), 0)
 
-        def load_weight(words, scales):
+        def load_words(words):
             nc.sync.dma_start(ww_raw[:].bitcast(I32), words.rearrange("o p n -> p o n").bitcast(I32))
+
+        def load_scales(raw, scales):
             for q in range(4):
-                nc.scalar.dma_start(
-                    ws_raw[32 * q : 32 * q + 4, :, :].bitcast(I32),
+                nc.sync.dma_start(
+                    raw[32 * q : 32 * q + 4, :, :].bitcast(I32),
                     scales[:, 4 * q : 4 * q + 4, :].rearrange("o r n -> r o n").bitcast(I32),
                 )
 
-        def deal_weight(name):
-            words = keep.tile([P, PACK, PASSES, 2 * P], U8, name=name + "_words", align_bytes=64)
-            scales = keep.tile([P, PACK, PASSES, P], U8, name=name + "_scales", align_bytes=64)
+        def deal_words(words):
             nc.vector.tensor_copy(
-                words[:].bitcast(U16).rearrange("p t o m -> p t (o m)").rearrange("p t (g i) -> p g t i", i=8),
+                words.bitcast(U16).rearrange("p t o m -> p t (o m)").rearrange("p t (g i) -> p g t i", i=8),
                 ww_raw[:].bitcast(U16).rearrange("p o n -> p (o n)").rearrange("p (g i t) -> p g t i", i=8, t=PACK),
             )
-            nc.vector.tensor_copy(
-                scales[:].rearrange("p t o m -> p t (o m)").rearrange("p t (g i) -> p g t i", i=16),
-                ws_raw[:].rearrange("p o n -> p (o n)").rearrange("p (g i t) -> p g t i", i=16, t=PACK),
-            )
-            return words, scales
 
-        load_weight(w1_words, w1_scales)
-        xw_win = [keep.tile([P, T], U32, name=f"xw_win{o}", align_bytes=64) for o in range(PASSES)]
+        def deal_scales(scales, raw):
+            nc.vector.tensor_copy(
+                scales.rearrange("p t o m -> p t (o m)").rearrange("p t (g i) -> p g t i", i=16),
+                raw[:].rearrange("p o n -> p (o n)").rearrange("p (g i t) -> p g t i", i=16, t=PACK),
+            )
+
+        xw_win = [keep.tile([P, T], U32, name=f"xw_win{o}", tag=f"xw_win{o}", align_bytes=64) for o in range(PASSES)]
         for o in range(PASSES):
             nc.sync.dma_start(xw_win[o][:].bitcast(I32), x_words[o].rearrange("p n t -> p (n t)").bitcast(I32))
+            if o == 0:
+                load_words(w1_words)
+                load_scales(ws_raw[0], w1_scales)
+        load_scales(ws_raw[1], w2_scales)
 
         xs_both = keep.tile([P, S], U8, name="xs_both", align_bytes=64)
         nc.vector.tensor_copy(xs_both[:], xs_win[:].indirect(offs_sb[:]))
-        nc.sync.dma_start(xs_second[0:100, :].bitcast(I32), xs_both[4:104, :].bitcast(I32))
-        x_planes = [xs_both, xs_second]
-
-        w1_dealt = deal_weight("w1")
-        load_weight(w2_words, w2_scales)
+        nc.sync.dma_start(x_planes[0][0:100, :].bitcast(I32), xs_both[24:124, :].bitcast(I32))
+        nc.sync.dma_start(x_planes[1][0:100, :].bitcast(I32), xs_both[28:128, :].bitcast(I32))
 
         xg = [[keep.tile([P, BANK], U32, name=f"xg{o}{h}", align_bytes=64) for h in range(HALVES)] for o in range(PASSES)]
-        for o in range(PASSES):
+
+        def gather_words(o):
             for h in range(HALVES):
                 cols = slice(h * BANK // 16, (h + 1) * BANK // 16)
                 nc.vector.tensor_copy(xg[o][h][:], xw_win[o][:].indirect(offs_sb[:, cols]))
 
-        w2_dealt = deal_weight("w2")
+        w1_dealt = (
+            keep.tile([P, PACK, PASSES, 2 * P], U8, name="w1_words_dealt", tag="xs_win", align_bytes=64),
+            keep.tile([P, PACK, PASSES, P], U8, name="w1_scales_dealt", tag="xw_win0", align_bytes=64),
+        )
+        deal_words(w1_dealt[0][:])
+        gather_words(0)
+        deal_scales(w1_dealt[1][:], ws_raw[0])
+        load_words(w2_words)
+        gather_words(1)
+        w2_both = keep.tile([P, 3 * PACK * PASSES * P], U8, name="w2_dealt", tag="xw_win1", align_bytes=64)
+        w2_dealt = (
+            w2_both[:, : 2 * PACK * PASSES * P].rearrange("p (t o m) -> p t o m", t=PACK, o=PASSES),
+            w2_both[:, 2 * PACK * PASSES * P :].rearrange("p (t o m) -> p t o m", t=PACK, o=PASSES),
+        )
+        deal_words(w2_dealt[0])
+        deal_scales(w2_dealt[1], ws_raw[1])
         nc.sync.dma_start(ww_raw[:, 0, 0 : 2 * N].bitcast(I32), w3_words[0].bitcast(I32))
         for q in range(4):
-            nc.sync.dma_start(ws_raw[32 * q : 32 * q + 4, 0, 0:N].bitcast(I32), w3_scales[0, 4 * q : 4 * q + 4, :].bitcast(I32))
+            nc.sync.dma_start(ws_raw[0][32 * q : 32 * q + 4, 0, 0:N].bitcast(I32), w3_scales[0, 4 * q : 4 * q + 4, :].bitcast(I32))
         nc.sync.dma_start(pix_sb[:], pix)
         unit_sb = keep.tile([P, PACK], F32, name="unit_sb")
         nc.gpsimd.dma_start(unit_sb[:], unit.rearrange("(p t) o -> p (t o)", t=PACK))
@@ -127,7 +147,7 @@ def tile_picked_yneusa_hit_p_kernel(
         picked = [keep.tile([P, PACK, PIX_HALF], BF16, name=f"picked{h}") for h in range(2)]
         woven = [keep.tile([P, PIX_HALF, PACK], BF16, name=f"woven{h}", align_bytes=64) for h in range(2)]
         rays = [slice(h * P, (h + 1) * P) for h in range(HALVES)]
-        recip, ratio, we, wf, ft, window, ray = {}, {}, {}, {}, {}, {}, {}
+        recip, ratio, we, wf, ft, window, ray, alf_pairs = {}, {}, {}, {}, {}, {}, {}, {}
 
         def shifted(vs, by):
             return slice(vs.start + by, vs.stop + by)
@@ -156,13 +176,21 @@ def tile_picked_yneusa_hit_p_kernel(
         def opacities(t, vs):
             nc.vector.scalar_tensor_tensor(alf[t % 2][:, :, shifted(vs, LEAD)], ratio[t][:, :, vs], 10.0, cdf[t % 2][:, :, vs], ALU.add, ALU.max)
 
-        def weights_and_hits(t):
+        def weights_inside(t):
             a = alf[t % 2]
-            alf_pairs = ring.tile([P, 2, V], F32, name="alf_pairs")
             nc.vector.scalar_tensor_tensor(we[t][:, 1:, :], a[:, : D - 1, LEAD:], -10.0, a[:, 1:, LEAD:], ALU.add, ALU.mult)
-            nc.vector.tensor_tensor(alf_pairs[:], a[:, 0:2, LEAD:], a[:, 2:4, LEAD:], ALU.max)
+
+        def weights_first(t):
+            a = alf[t % 2]
             nc.vector.scalar_tensor_tensor(we[t][:, 0, :], a[:, D - 1, LEAD - 1 : LEAD - 1 + V], -10.0, a[:, 0, LEAD:], ALU.add, ALU.mult)
-            nc.vector.tensor_tensor(window[t][:, V:], alf_pairs[:, 0, :], alf_pairs[:, 1, :], ALU.max)
+
+        def largest_of_pairs(t):
+            a = alf[t % 2]
+            alf_pairs[t] = ring.tile([P, 2, V], F32, name="alf_pairs")
+            nc.vector.tensor_tensor(alf_pairs[t][:], a[:, 0:2, LEAD:], a[:, 2:4, LEAD:], ALU.max)
+
+        def hits(t):
+            nc.vector.tensor_tensor(window[t][:, V:], alf_pairs[t][:, 0, :], alf_pairs[t][:, 1, :], ALU.max)
 
         def weighted(t, h):
             nc.vector.tensor_tensor(wf[t][:, h], ft[t][h], we[t][:, :, rays[h]], ALU.mult)
@@ -178,8 +206,10 @@ def tile_picked_yneusa_hit_p_kernel(
             for h in range(HALVES):
                 nc.tensor.transpose(ray[t][:, rays[h]], turned_sb[:, h, :], ident[:])
 
+        def shade(t, sums, vs):
+            nc.vector.scalar_tensor_tensor(window[t][:, vs], sums, gain[:, t : t + 1], window[t][:, shifted(vs, V)], ALU.mult, ALU.mult)
+
         def look_up(t):
-            nc.vector.scalar_tensor_tensor(window[t][:, :V], ray[t][:], gain[:, t : t + 1], window[t][:, V:], ALU.mult, ALU.mult)
             for h in range(2):
                 looked_up = window[t][:].indirect(pix_sb[:, h * PIX_HALF // 16 : (h + 1) * PIX_HALF // 16])
                 if t == PACK - 1 and h == 0:
@@ -195,9 +225,7 @@ def tile_picked_yneusa_hit_p_kernel(
             if t == 0:
                 for h in range(HALVES):
                     nc.vector.tensor_scalar(recip[t][:, :, rays[h]], far[:, :, rays[h]], -10.0 * RATIO, -RATIO, ALU.mult, ALU.add)
-                for h in range(HALVES):
                     ratios(t, rays[h])
-                for h in range(HALVES):
                     opacities(t, rays[h])
             else:
                 ratios(t, slice(0, V))
@@ -205,41 +233,54 @@ def tile_picked_yneusa_hit_p_kernel(
                 opacities(t, slice(0, V))
                 weighted(t - 1, 1)
                 ray_sums_on_tensor(t - 1)
-            weights_and_hits(t)
-            if 0 < t < PACK - 1:
-                look_up(t - 1)
+            weights_inside(t)
+            if t < PACK - 1:
+                largest_of_pairs(t)
+                weights_first(t)
+                hits(t)
+                if t > 0:
+                    shade(t - 1, ray[t - 1][:], slice(0, V))
+                    look_up(t - 1)
         last = PACK - 1
-        weighted(last, 0)
-        weighted(last, 1)
+        largest_of_pairs(last)
+        weights_first(last)
+        shade(last - 1, ray[last - 1][:], slice(0, V))
         look_up(last - 1)
         wf_pairs = keep.tile([P, HALVES, 2, P], F32, name="wf_pairs")
-        nc.vector.tensor_tensor(wf_pairs[:], wf[last][:, :, 0:2, :], wf[last][:, :, 2:4, :], ALU.add)
-        ray[last] = keep.tile([P, V], F32, name="ray_last")
-        nc.vector.tensor_tensor(ray[last][:].rearrange("p (h v) -> p h v", h=HALVES), wf_pairs[:, :, 0, :], wf_pairs[:, :, 1, :], ALU.add)
+        ray_last = keep.tile([P, V], F32, name="ray_last")
+        for h in range(HALVES):
+            weighted(last, h)
+        for h in range(HALVES):
+            nc.vector.tensor_tensor(wf_pairs[:, h], wf[last][:, h, 0:2, :], wf[last][:, h, 2:4, :], ALU.add)
+            if h == 0:
+                hits(last)
+        for h in range(HALVES):
+            nc.vector.tensor_tensor(ray_last[:, rays[h]], wf_pairs[:, h, 0, :], wf_pairs[:, h, 1, :], ALU.add)
+        for h in range(HALVES):
+            shade(last, ray_last[:, rays[h]], rays[h])
         look_up(last)
 
-        out_view = out.rearrange("(m p) r -> p m r", p=P)
         codes = [keep.tile([P, PIX_HALF], U32, name=f"codes{h}", align_bytes=64) for h in range(2)]
         planes = [keep.tile([P, PIX_HALF], U8, name=f"planes{h}", align_bytes=64) for h in range(2)]
         nc.vector.tensor_copy(woven[0][:, :, 2:4], picked[0][:, 2:4, :].rearrange("p t r -> p r t"))
         nc.scalar.copy(woven[1][:, :, 2:4], picked[1][:, 2:4, :].rearrange("p t r -> p r t"))
         for h in range(2):
             nc.vector.quantize_mx(out=codes[h][:].bitcast(FP8X4), scales=planes[h][:], in_=woven[h][:].rearrange("p r t -> p (r t)"))
-            acc = psum.tile([P, BANK], F32, name="sd", bufs=4)
             for m in range(N // P):
+                acc = psum.tile([P, BANK], F32, name="sd", bufs=4)
                 nc.tensor.matmul_mx(
-                    out=acc[:, m * PIX_HALF : (m + 1) * PIX_HALF],
+                    out=acc[:, :PIX_HALF],
                     lhsT=ww_raw[:, 0, 2 * P * m : 2 * P * (m + 1)].bitcast(FP4X4),
-                    lhsT_scale=ws_raw[:, 0, P * m : P * (m + 1)],
+                    lhsT_scale=ws_raw[0][:, 0, P * m : P * (m + 1)],
                     rhs=codes[h][:].bitcast(FP8X4),
                     rhs_scale=planes[h][:],
                     start=True,
                     stop=True,
                 )
-            result = keep.tile([P, N // P, PIX_HALF], F32, name=f"result{h}")
-            if h == 0:
-                nc.scalar.copy(result[:].rearrange("p m r -> p (m r)"), acc[:])
-                nc.scalar.dma_start(out_view[:, :, 0:PIX_HALF], result[:])
-            else:
-                nc.vector.tensor_copy(result[:].rearrange("p m r -> p (m r)"), acc[:])
-                nc.sync.dma_start(out_view[:, :, PIX_HALF:], result[:])
+                result = keep.tile([P, PIX_HALF], F32, name=f"result{h}{m}")
+                target = out[m * P : (m + 1) * P, h * PIX_HALF : (h + 1) * PIX_HALF]
+                if h == 1 and m == 1:
+                    nc.vector.tensor_copy(result[:], acc[:, :PIX_HALF])
+                else:
+                    nc.scalar.copy(result[:], acc[:, :PIX_HALF])
+                nc.sync.dma_start(target, result[:])

@@ -121,10 +121,11 @@ def tile_picked_yneusa_hit_p_kernel(
         gain = keep.tile([P, PACK], F32, name="gain")
         nc.gpsimd.tensor_scalar(gain[:], unit_sb[:], -0.001, 0.0, ALU.mult, ALU.add)
 
-        cdf = [keep.tile([P, D, V + LEAD], F32, name=f"cdf{b}") for b in range(2)]
+        cdf = [keep.tile([P, D, V + LEAD], F32, name=f"cdf{b}") for b in range(PACK)]
         alf = [keep.tile([P, D, LEAD + V], F32, name=f"alf{b}") for b in range(2)]
-        for b in range(2):
+        for b in range(PACK):
             nc.gpsimd.memset(cdf[b][:, 0, V : V + 1], 0.0)
+        for b in range(2):
             nc.gpsimd.memset(alf[b][:, D - 1, LEAD - 1 : LEAD], 10.0)
         ident = keep.tile([P, P], F32, name="ident")
         make_identity(nc, ident[:])
@@ -154,14 +155,14 @@ def tile_picked_yneusa_hit_p_kernel(
 
         def sigmoids(t):
             far = ring.tile([P, D, V], F32, name="far")
-            recip[t] = ring.tile([P, D, V], F32, name="recip")
+            recip[t] = ring.tile([P, D, V], F32, name="recip", bufs=PACK)
             for h in range(HALVES):
-                sd = product(w1_dealt, t, h, "sd", 4)
-                nc.scalar.activation(cdf[t % 2][:, :, rays[h]], sd, ACT.Sigmoid, scale=2.5)
+                sd = product(w1_dealt, t, h, "sd", 3)
+                nc.scalar.activation(cdf[t][:, :, rays[h]], sd, ACT.Sigmoid, scale=2.5)
                 nc.scalar.activation(far[:, :, rays[h]], sd, ACT.Sigmoid, scale=-2.5, bias=-math.log(11.0))
                 if t > 0:
                     nc.scalar.activation(recip[t][:, :, rays[h]], far[:, :, rays[h]], ACT.Copy, scale=-10.0 * RATIO, bias=-RATIO)
-            ft[t] = [product(w2_dealt, t, h, "ft", 2) for h in range(HALVES)]
+            ft[t] = [product(w2_dealt, t, h, "ft", 3) for h in range(HALVES)]
             ratio[t] = ring.tile([P, D, V], F32, name="ratio")
             we[t] = ring.tile([P, D, V], F32, name="we")
             wf[t] = ring.tile([P, HALVES, D, P], F32, name="wf")
@@ -169,12 +170,12 @@ def tile_picked_yneusa_hit_p_kernel(
             return far
 
         def ratios(t, vs):
-            c = cdf[t % 2]
+            c = cdf[t]
             nc.vector.scalar_tensor_tensor(ratio[t][:, : D - 1, vs], c[:, 1:, vs], 0.1, recip[t][:, : D - 1, vs], ALU.add, ALU.mult)
             nc.vector.scalar_tensor_tensor(ratio[t][:, D - 1, vs], c[:, 0, shifted(vs, 1)], 0.1, recip[t][:, D - 1, vs], ALU.add, ALU.mult)
 
         def opacities(t, vs):
-            nc.vector.scalar_tensor_tensor(alf[t % 2][:, :, shifted(vs, LEAD)], ratio[t][:, :, vs], 10.0, cdf[t % 2][:, :, vs], ALU.add, ALU.max)
+            nc.vector.scalar_tensor_tensor(alf[t % 2][:, :, shifted(vs, LEAD)], ratio[t][:, :, vs], 10.0, cdf[t][:, :, vs], ALU.add, ALU.max)
 
         def weights_inside(t):
             a = alf[t % 2]
@@ -229,6 +230,9 @@ def tile_picked_yneusa_hit_p_kernel(
                     opacities(t, rays[h])
             else:
                 ratios(t, slice(0, V))
+                if t >= 2:
+                    shade(t - 2, ray[t - 2][:], slice(0, V))
+                    look_up(t - 2)
                 weighted(t - 1, 0)
                 opacities(t, slice(0, V))
                 weighted(t - 1, 1)
@@ -238,18 +242,15 @@ def tile_picked_yneusa_hit_p_kernel(
                 largest_of_pairs(t)
                 weights_first(t)
                 hits(t)
-                if t > 0:
-                    shade(t - 1, ray[t - 1][:], slice(0, V))
-                    look_up(t - 1)
         last = PACK - 1
         largest_of_pairs(last)
         weights_first(last)
-        shade(last - 1, ray[last - 1][:], slice(0, V))
-        look_up(last - 1)
         wf_pairs = keep.tile([P, HALVES, 2, P], F32, name="wf_pairs")
         ray_last = keep.tile([P, V], F32, name="ray_last")
         for h in range(HALVES):
             weighted(last, h)
+        shade(last - 1, ray[last - 1][:], slice(0, V))
+        look_up(last - 1)
         for h in range(HALVES):
             nc.vector.tensor_tensor(wf_pairs[:, h], wf[last][:, h, 0:2, :], wf[last][:, h, 2:4, :], ALU.add)
             if h == 0:
@@ -267,7 +268,7 @@ def tile_picked_yneusa_hit_p_kernel(
         for h in range(2):
             nc.vector.quantize_mx(out=codes[h][:].bitcast(FP8X4), scales=planes[h][:], in_=woven[h][:].rearrange("p r t -> p (r t)"))
             for m in range(N // P):
-                acc = psum.tile([P, BANK], F32, name="sd", bufs=4)
+                acc = psum.tile([P, BANK], F32, name="sd", bufs=3)
                 nc.tensor.matmul_mx(
                     out=acc[:, :PIX_HALF],
                     lhsT=ww_raw[:, 0, 2 * P * m : 2 * P * (m + 1)].bitcast(FP4X4),

@@ -143,7 +143,7 @@ def tile_picked_yneusa_hit_p_kernel(
                     start=(o == 0),
                     stop=(o == PASSES - 1),
                 )
-            return acc[:].rearrange("p (v d) -> p d v", d=D)
+            return acc[:].rearrange("p (g i d) -> p g d i", i=4, d=D)
 
         picked = [keep.tile([P, PACK, PIX_HALF], BF16, name=f"picked{h}") for h in range(2)]
         woven = [keep.tile([P, PIX_HALF, PACK], BF16, name=f"woven{h}", align_bytes=64) for h in range(2)]
@@ -153,13 +153,16 @@ def tile_picked_yneusa_hit_p_kernel(
         def shifted(vs, by):
             return slice(vs.start + by, vs.stop + by)
 
+        def by_lines(view):
+            return view.rearrange("p d (g i) -> p g d i", i=4)
+
         def sigmoids(t):
             far = ring.tile([P, D, V], F32, name="far")
             recip[t] = ring.tile([P, D, V], F32, name="recip", bufs=PACK)
             for h in range(HALVES):
                 sd = product(w1_dealt, t, h, "sd", 3)
-                nc.scalar.activation(cdf[t][:, :, rays[h]], sd, ACT.Sigmoid, scale=2.5)
-                nc.scalar.activation(far[:, :, rays[h]], sd, ACT.Sigmoid, scale=-2.5, bias=-math.log(11.0))
+                nc.scalar.activation(by_lines(cdf[t][:, :, rays[h]]), sd, ACT.Sigmoid, scale=2.5)
+                nc.scalar.activation(by_lines(far[:, :, rays[h]]), sd, ACT.Sigmoid, scale=-2.5, bias=-math.log(11.0))
                 if t > 0:
                     nc.scalar.activation(recip[t][:, :, rays[h]], far[:, :, rays[h]], ACT.Copy, scale=-10.0 * RATIO, bias=-RATIO)
             ft[t] = [product(w2_dealt, t, h, "ft", 3) for h in range(HALVES)]
@@ -194,7 +197,7 @@ def tile_picked_yneusa_hit_p_kernel(
             nc.vector.tensor_tensor(window[t][:, V:], alf_pairs[t][:, 0, :], alf_pairs[t][:, 1, :], ALU.max)
 
         def weighted(t, h):
-            nc.vector.tensor_tensor(wf[t][:, h], ft[t][h], we[t][:, :, rays[h]], ALU.mult)
+            nc.vector.tensor_tensor(by_lines(wf[t][:, h]), ft[t][h], by_lines(we[t][:, :, rays[h]]), ALU.mult)
 
         def ray_sums_on_tensor(t):
             turned = psum.tile([P, HALVES, P], F32, name="turned", bufs=1)

@@ -42,7 +42,7 @@ def tile_picked_yneusa_hit_p_kernel(
         nc.sync.dma_start(offs_sb[:], offs)
 
         xs_win = keep.tile([P, T], U8, name="xs_win", tag="xs_win", align_bytes=64)
-        ws_raw = [keep.tile([P, PASSES, H], U8, name=f"ws_raw{w}", align_bytes=64) for w in range(2)]
+        ws_raw = [keep.tile([P, PASSES, H], U8, name=f"ws_raw{w}", tag=f"ws_raw{w}", align_bytes=64) for w in range(2)]
         ww_raw = keep.tile([P, PASSES, 2 * H], U8, name="ww_raw", align_bytes=64)
         x_planes = [keep.tile([P, S], U8, name=f"x_plane{o}", align_bytes=64) for o in range(PASSES)]
         for q in range(4):
@@ -50,7 +50,7 @@ def tile_picked_yneusa_hit_p_kernel(
         for w in range(2):
             nc.gpsimd.memset(ws_raw[w][:].bitcast(I32), 0)
         for q in range(4):
-            (nc.vector if q % 2 else nc.gpsimd).memset(xs_win[32 * q : 32 * q + 24, :].bitcast(I32), 0)
+            nc.vector.memset(xs_win[32 * q : 32 * q + 24, :].bitcast(I32), 0)
         for o in range(PASSES):
             nc.gpsimd.memset(x_planes[o][96:128, :].bitcast(I32), 0)
 
@@ -116,10 +116,10 @@ def tile_picked_yneusa_hit_p_kernel(
         for q in range(4):
             nc.sync.dma_start(ws_raw[0][32 * q : 32 * q + 4, 0, 0:N].bitcast(I32), w3_scales[0, 4 * q : 4 * q + 4, :].bitcast(I32))
         nc.sync.dma_start(pix_sb[:], pix)
-        unit_sb = keep.tile([P, PACK], F32, name="unit_sb")
-        nc.gpsimd.dma_start(unit_sb[:], unit.rearrange("(p t) o -> p (t o)", t=PACK))
+        unit_sb = keep.tile([P, PACK], F32, name="unit_sb", tag="ws_raw1", align_bytes=64)
+        nc.sync.dma_start(unit_sb[:], unit.rearrange("(p t) o -> p (t o)", t=PACK))
         gain = keep.tile([P, PACK], F32, name="gain")
-        nc.gpsimd.tensor_scalar(gain[:], unit_sb[:], -0.001, 0.0, ALU.mult, ALU.add)
+        nc.scalar.activation(gain[:], unit_sb[:], ACT.Copy, scale=-0.001)
 
         cdf = [keep.tile([P, D, V + LEAD], F32, name=f"cdf{b}") for b in range(PACK)]
         alf = [keep.tile([P, D, LEAD + V], F32, name=f"alf{b}") for b in range(2)]
@@ -148,6 +148,8 @@ def tile_picked_yneusa_hit_p_kernel(
         picked = [keep.tile([P, PACK, PIX_HALF], BF16, name=f"picked{h}") for h in range(2)]
         woven = [keep.tile([P, PIX_HALF, PACK], BF16, name=f"woven{h}", align_bytes=64) for h in range(2)]
         rays = [slice(h * P, (h + 1) * P) for h in range(HALVES)]
+        every_ray = slice(0, V)
+        last = PACK - 1
         recip, ratio, we, wf, ft, window, ray, alf_pairs = {}, {}, {}, {}, {}, {}, {}, {}
 
         def shifted(vs, by):
@@ -169,6 +171,7 @@ def tile_picked_yneusa_hit_p_kernel(
             ratio[t] = ring.tile([P, D, V], F32, name="ratio")
             we[t] = ring.tile([P, D, V], F32, name="we")
             wf[t] = ring.tile([P, HALVES, D, P], F32, name="wf")
+            alf_pairs[t] = ring.tile([P, 2, V], F32, name="alf_pairs")
             window[t] = ring.tile([P, 2 * V], F32, name="window", bufs=4)
             return far
 
@@ -180,18 +183,17 @@ def tile_picked_yneusa_hit_p_kernel(
         def opacities(t, vs):
             nc.vector.scalar_tensor_tensor(alf[t % 2][:, :, shifted(vs, LEAD)], ratio[t][:, :, vs], 10.0, cdf[t][:, :, vs], ALU.add, ALU.max)
 
-        def weights_inside(t):
-            a = alf[t % 2]
-            nc.vector.scalar_tensor_tensor(we[t][:, 1:, :], a[:, : D - 1, LEAD:], -10.0, a[:, 1:, LEAD:], ALU.add, ALU.mult)
+        def weights_inside(t, vs):
+            a, here = alf[t % 2], shifted(vs, LEAD)
+            nc.vector.scalar_tensor_tensor(we[t][:, 1:, vs], a[:, : D - 1, here], -10.0, a[:, 1:, here], ALU.add, ALU.mult)
 
         def weights_first(t):
             a = alf[t % 2]
             nc.vector.scalar_tensor_tensor(we[t][:, 0, :], a[:, D - 1, LEAD - 1 : LEAD - 1 + V], -10.0, a[:, 0, LEAD:], ALU.add, ALU.mult)
 
-        def largest_of_pairs(t):
-            a = alf[t % 2]
-            alf_pairs[t] = ring.tile([P, 2, V], F32, name="alf_pairs")
-            nc.vector.tensor_tensor(alf_pairs[t][:], a[:, 0:2, LEAD:], a[:, 2:4, LEAD:], ALU.max)
+        def largest_of_pairs_in(t, vs):
+            a, here = alf[t % 2], shifted(vs, LEAD)
+            nc.vector.tensor_tensor(alf_pairs[t][:, :, vs], a[:, 0:2, here], a[:, 2:4, here], ALU.max)
 
         def hits(t):
             nc.vector.tensor_tensor(window[t][:, V:], alf_pairs[t][:, 0, :], alf_pairs[t][:, 1, :], ALU.max)
@@ -213,13 +215,12 @@ def tile_picked_yneusa_hit_p_kernel(
         def shade(t, sums, vs):
             nc.vector.scalar_tensor_tensor(window[t][:, vs], sums, gain[:, t : t + 1], window[t][:, shifted(vs, V)], ALU.mult, ALU.mult)
 
+        def by_pixel(t, first, count):
+            return window[t][:].indirect(pix_sb[:, first // 16 : (first + count) // 16])
+
         def look_up(t):
             for h in range(2):
-                looked_up = window[t][:].indirect(pix_sb[:, h * PIX_HALF // 16 : (h + 1) * PIX_HALF // 16])
-                if t == PACK - 1 and h == 0:
-                    nc.vector.tensor_copy(picked[h][:, t, :], looked_up)
-                else:
-                    nc.scalar.activation(picked[h][:, t, :], looked_up, ACT.Copy)
+                nc.scalar.activation(picked[h][:, t, :], by_pixel(t, h * PIX_HALF, PIX_HALF), ACT.Copy)
             if t == 1:
                 for h in range(2):
                     nc.scalar.copy(woven[h][:, :, 0:2], picked[h][:, 0:2, :].rearrange("p t r -> p r t"))
@@ -229,31 +230,36 @@ def tile_picked_yneusa_hit_p_kernel(
             if t == 0:
                 for h in range(HALVES):
                     nc.vector.tensor_scalar(recip[t][:, :, rays[h]], far[:, :, rays[h]], -10.0 * RATIO, -RATIO, ALU.mult, ALU.add)
+                    if h == 1:
+                        opacities(t, rays[0])
                     ratios(t, rays[h])
-                    opacities(t, rays[h])
+                weights_inside(t, rays[0])
+                opacities(t, rays[1])
+                largest_of_pairs_in(t, rays[0])
+                weights_inside(t, rays[1])
+                largest_of_pairs_in(t, rays[1])
             else:
-                ratios(t, slice(0, V))
+                ratios(t, every_ray)
                 if t >= 2:
-                    shade(t - 2, ray[t - 2][:], slice(0, V))
+                    shade(t - 2, ray[t - 2][:], every_ray)
                     look_up(t - 2)
                 weighted(t - 1, 0)
-                opacities(t, slice(0, V))
+                opacities(t, every_ray)
                 weighted(t - 1, 1)
                 ray_sums_on_tensor(t - 1)
-            weights_inside(t)
-            if t < PACK - 1:
-                largest_of_pairs(t)
-                weights_first(t)
+                weights_inside(t, every_ray)
+                if t < last:
+                    largest_of_pairs_in(t, every_ray)
+            weights_first(t)
+            if t < last:
                 hits(t)
-        last = PACK - 1
-        largest_of_pairs(last)
-        weights_first(last)
+        largest_of_pairs_in(last, every_ray)
+        weighted(last, 0)
+        shade(last - 1, ray[last - 1][:], every_ray)
+        look_up(last - 1)
+        weighted(last, 1)
         wf_pairs = keep.tile([P, HALVES, 2, P], F32, name="wf_pairs")
         ray_last = keep.tile([P, V], F32, name="ray_last")
-        for h in range(HALVES):
-            weighted(last, h)
-        shade(last - 1, ray[last - 1][:], slice(0, V))
-        look_up(last - 1)
         for h in range(HALVES):
             nc.vector.tensor_tensor(wf_pairs[:, h], wf[last][:, h, 0:2, :], wf[last][:, h, 2:4, :], ALU.add)
             if h == 0:
@@ -262,11 +268,15 @@ def tile_picked_yneusa_hit_p_kernel(
             nc.vector.tensor_tensor(ray_last[:, rays[h]], wf_pairs[:, h, 0, :], wf_pairs[:, h, 1, :], ALU.add)
         for h in range(HALVES):
             shade(last, ray_last[:, rays[h]], rays[h])
-        look_up(last)
+        quarters = [slice(0, PIX_HALF // 2), slice(PIX_HALF // 2, PIX_HALF)]
+        for rs in quarters:
+            nc.vector.tensor_copy(picked[0][:, last, rs], by_pixel(last, rs.start, PIX_HALF // 2))
+        nc.scalar.activation(picked[1][:, last, :], by_pixel(last, PIX_HALF, PIX_HALF), ACT.Copy)
 
         codes = [keep.tile([P, PIX_HALF], U32, name=f"codes{h}", align_bytes=64) for h in range(2)]
         planes = [keep.tile([P, PIX_HALF], U8, name=f"planes{h}", align_bytes=64) for h in range(2)]
-        nc.vector.tensor_copy(woven[0][:, :, 2:4], picked[0][:, 2:4, :].rearrange("p t r -> p r t"))
+        for rs in quarters:
+            nc.vector.tensor_copy(woven[0][:, rs, 2:4], picked[0][:, 2:4, rs].rearrange("p t r -> p r t"))
         nc.scalar.copy(woven[1][:, :, 2:4], picked[1][:, 2:4, :].rearrange("p t r -> p r t"))
         for h in range(2):
             nc.vector.quantize_mx(out=codes[h][:].bitcast(FP8X4), scales=planes[h][:], in_=woven[h][:].rearrange("p r t -> p (r t)"))

import math
from contextlib import ExitStack

import concourse.mybir as mybir
from concourse.masks import make_identity

K, T, S, D, N, H, V, U = 1024, 2048, 1024, 4, 256, 512, 256, 512
FLOPS = 2 * (2 * K * H * S + H * N * U)

F32 = mybir.dt.float32
BF16 = mybir.dt.bfloat16
I32 = mybir.dt.int32
U32 = mybir.dt.uint32
U16 = mybir.dt.uint16
U8 = mybir.dt.uint8
FP8X4 = mybir.dt.float8_e4m3fn_x4
FP4X4 = mybir.dt.float4_e2m1fn_x4
ALU = mybir.AluOpType
ACT = mybir.ActivationFunctionType

P = 128
PACK = 4
PASSES = K // (P * PACK)
BANK = 512
HALVES = S // BANK
PIX_HALF = U // 2
LEAD = 8
RATIO = 100.0 / 11.0


def tile_picked_yneusa_hit_p_kernel(
    tc, x_words, x_scales, w1_words, w1_scales, w2_words, w2_scales, unit, w3_words, w3_scales, offs, pix, out
):
    nc = tc.nc
    with ExitStack() as ctx:
        keep = ctx.enter_context(tc.tile_pool(name="keep", bufs=1))
        ring = ctx.enter_context(tc.tile_pool(name="ring", bufs=2))
        psum = ctx.enter_context(tc.psum_pool(name="psum", bufs=1))

        offs_sb = keep.tile([P, S // 16], U16, name="offs_sb")
        pix_sb = keep.tile([P, U // 16], U16, name="pix_sb")
        nc.sync.dma_start(offs_sb[:], offs)

        xs_win = keep.tile([P, T], U8, name="xs_win", tag="xs_win", align_bytes=64)
        ws_raw = [keep.tile([P, PASSES, H], U8, name=f"ws_raw{w}", tag=f"ws_raw{w}", align_bytes=64) for w in range(2)]
        ww_raw = keep.tile([P, PASSES, 2 * H], U8, name="ww_raw", align_bytes=64)
        x_planes = [keep.tile([P, S], U8, name=f"x_plane{o}", align_bytes=64) for o in range(PASSES)]
        for q in range(4):
            nc.sync.dma_start(xs_win[32 * q + 24 : 32 * q + 32, :].bitcast(I32), x_scales[:, 4 * q : 4 * q + 4, :].bitcast(I32))
        for w in range(2):
            nc.gpsimd.memset(ws_raw[w][:].bitcast(I32), 0)
        for q in range(4):
            nc.vector.memset(xs_win[32 * q : 32 * q + 24, :].bitcast(I32), 0)
        for o in range(PASSES):
            nc.gpsimd.memset(x_planes[o][96:128, :].bitcast(I32), 0)

        def load_words(words):
            nc.sync.dma_start(ww_raw[:].bitcast(I32), words.rearrange("o p n -> p o n").bitcast(I32))

        def load_scales(raw, scales):
            for q in range(4):
                nc.sync.dma_start(
                    raw[32 * q : 32 * q + 4, :, :].bitcast(I32),
                    scales[:, 4 * q : 4 * q + 4, :].rearrange("o r n -> r o n").bitcast(I32),
                )

        def deal_words(words):
            nc.vector.tensor_copy(
                words.bitcast(U16).rearrange("p t o m -> p t (o m)").rearrange("p t (g i) -> p g t i", i=8),
                ww_raw[:].bitcast(U16).rearrange("p o n -> p (o n)").rearrange("p (g i t) -> p g t i", i=8, t=PACK),
            )

        def deal_scales(scales, raw):
            nc.vector.tensor_copy(
                scales.rearrange("p t o m -> p t (o m)").rearrange("p t (g i) -> p g t i", i=16),
                raw[:].rearrange("p o n -> p (o n)").rearrange("p (g i t) -> p g t i", i=16, t=PACK),
            )

        xw_win = [keep.tile([P, T], U32, name=f"xw_win{o}", tag=f"xw_win{o}", align_bytes=64) for o in range(PASSES)]
        for o in range(PASSES):
            nc.sync.dma_start(xw_win[o][:].bitcast(I32), x_words[o].rearrange("p n t -> p (n t)").bitcast(I32))
            if o == 0:
                load_words(w1_words)
                load_scales(ws_raw[0], w1_scales)
        load_scales(ws_raw[1], w2_scales)

        xs_both = keep.tile([P, S], U8, name="xs_both", align_bytes=64)
        nc.vector.tensor_copy(xs_both[:], xs_win[:].indirect(offs_sb[:]))
        nc.sync.dma_start(x_planes[0][0:100, :].bitcast(I32), xs_both[24:124, :].bitcast(I32))
        nc.sync.dma_start(x_planes[1][0:100, :].bitcast(I32), xs_both[28:128, :].bitcast(I32))

        xg = [[keep.tile([P, BANK], U32, name=f"xg{o}{h}", align_bytes=64) for h in range(HALVES)] for o in range(PASSES)]

        def gather_words(o):
            for h in range(HALVES):
                cols = slice(h * BANK // 16, (h + 1) * BANK // 16)
                nc.vector.tensor_copy(xg[o][h][:], xw_win[o][:].indirect(offs_sb[:, cols]))

        w1_dealt = (
            keep.tile([P, PACK, PASSES, 2 * P], U8, name="w1_words_dealt", tag="xs_win", align_bytes=64),
            keep.tile([P, PACK, PASSES, P], U8, name="w1_scales_dealt", tag="xw_win0", align_bytes=64),
        )
        deal_words(w1_dealt[0][:])
        gather_words(0)
        deal_scales(w1_dealt[1][:], ws_raw[0])
        load_words(w2_words)
        gather_words(1)
        w2_both = keep.tile([P, 3 * PACK * PASSES * P], U8, name="w2_dealt", tag="xw_win1", align_bytes=64)
        w2_dealt = (
            w2_both[:, : 2 * PACK * PASSES * P].rearrange("p (t o m) -> p t o m", t=PACK, o=PASSES),
            w2_both[:, 2 * PACK * PASSES * P :].rearrange("p (t o m) -> p t o m", t=PACK, o=PASSES),
        )
        deal_words(w2_dealt[0])
        deal_scales(w2_dealt[1], ws_raw[1])
        nc.sync.dma_start(ww_raw[:, 0, 0 : 2 * N].bitcast(I32), w3_words[0].bitcast(I32))
        for q in range(4):
            nc.sync.dma_start(ws_raw[0][32 * q : 32 * q + 4, 0, 0:N].bitcast(I32), w3_scales[0, 4 * q : 4 * q + 4, :].bitcast(I32))
        nc.sync.dma_start(pix_sb[:], pix)
        unit_sb = keep.tile([P, PACK], F32, name="unit_sb", tag="ws_raw1", align_bytes=64)
        nc.sync.dma_start(unit_sb[:], unit.rearrange("(p t) o -> p (t o)", t=PACK))
        gain = keep.tile([P, PACK], F32, name="gain")
        nc.scalar.activation(gain[:], unit_sb[:], ACT.Copy, scale=-0.001)

        cdf = [keep.tile([P, D, V + LEAD], F32, name=f"cdf{b}") for b in range(PACK)]
        alf = [keep.tile([P, D, LEAD + V], F32, name=f"alf{b}") for b in range(2)]
        for b in range(PACK):
            nc.gpsimd.memset(cdf[b][:, 0, V : V + 1], 0.0)
        for b in range(2):
            nc.gpsimd.memset(alf[b][:, D - 1, LEAD - 1 : LEAD], 10.0)
        ident = keep.tile([P, P], F32, name="ident")
        make_identity(nc, ident[:])

        def product(dealt, t, h, tag, bufs):
            words, scales = dealt
            acc = psum.tile([P, BANK], F32, name=tag, bufs=bufs)
            for o in range(PASSES):
                nc.tensor.matmul_mx(
                    out=acc[:],
                    lhsT=words[:, t, o, :].bitcast(FP4X4),
                    lhsT_scale=scales[:, t, o, :],
                    rhs=xg[o][h][:].bitcast(FP8X4),
                    rhs_scale=x_planes[o][:, h * BANK : (h + 1) * BANK],
                    start=(o == 0),
                    stop=(o == PASSES - 1),
                )
            return acc[:].rearrange("p (g i d) -> p g d i", i=4, d=D)

        picked = [keep.tile([P, PACK, PIX_HALF], BF16, name=f"picked{h}") for h in range(2)]
        woven = [keep.tile([P, PIX_HALF, PACK], BF16, name=f"woven{h}", align_bytes=64) for h in range(2)]
        rays = [slice(h * P, (h + 1) * P) for h in range(HALVES)]
        every_ray = slice(0, V)
        last = PACK - 1
        recip, ratio, we, wf, ft, window, ray, alf_pairs = {}, {}, {}, {}, {}, {}, {}, {}

        def shifted(vs, by):
            return slice(vs.start + by, vs.stop + by)

        def by_lines(view):
            return view.rearrange("p d (g i) -> p g d i", i=4)

        def sigmoids(t):
            far = ring.tile([P, D, V], F32, name="far")
            recip[t] = ring.tile([P, D, V], F32, name="recip", bufs=PACK)
            for h in range(HALVES):
                sd = product(w1_dealt, t, h, "sd", 3)
                nc.scalar.activation(by_lines(cdf[t][:, :, rays[h]]), sd, ACT.Sigmoid, scale=2.5)
                nc.scalar.activation(by_lines(far[:, :, rays[h]]), sd, ACT.Sigmoid, scale=-2.5, bias=-math.log(11.0))
                if t > 0:
                    nc.scalar.activation(recip[t][:, :, rays[h]], far[:, :, rays[h]], ACT.Copy, scale=-10.0 * RATIO, bias=-RATIO)
            ft[t] = [product(w2_dealt, t, h, "ft", 3) for h in range(HALVES)]
            ratio[t] = ring.tile([P, D, V], F32, name="ratio")
            we[t] = ring.tile([P, D, V], F32, name="we")
            wf[t] = ring.tile([P, HALVES, D, P], F32, name="wf")
            alf_pairs[t] = ring.tile([P, 2, V], F32, name="alf_pairs")
            window[t] = ring.tile([P, 2 * V], F32, name="window", bufs=4)
            return far

        def ratios(t, vs):
            c = cdf[t]
            nc.vector.scalar_tensor_tensor(ratio[t][:, : D - 1, vs], c[:, 1:, vs], 0.1, recip[t][:, : D - 1, vs], ALU.add, ALU.mult)
            nc.vector.scalar_tensor_tensor(ratio[t][:, D - 1, vs], c[:, 0, shifted(vs, 1)], 0.1, recip[t][:, D - 1, vs], ALU.add, ALU.mult)

        def opacities(t, vs):
            nc.vector.scalar_tensor_tensor(alf[t % 2][:, :, shifted(vs, LEAD)], ratio[t][:, :, vs], 10.0, cdf[t][:, :, vs], ALU.add, ALU.max)

        def weights_inside(t, vs):
            a, here = alf[t % 2], shifted(vs, LEAD)
            nc.vector.scalar_tensor_tensor(we[t][:, 1:, vs], a[:, : D - 1, here], -10.0, a[:, 1:, here], ALU.add, ALU.mult)

        def weights_first(t):
            a = alf[t % 2]
            nc.vector.scalar_tensor_tensor(we[t][:, 0, :], a[:, D - 1, LEAD - 1 : LEAD - 1 + V], -10.0, a[:, 0, LEAD:], ALU.add, ALU.mult)

        def largest_of_pairs_in(t, vs):
            a, here = alf[t % 2], shifted(vs, LEAD)
            nc.vector.tensor_tensor(alf_pairs[t][:, :, vs], a[:, 0:2, here], a[:, 2:4, here], ALU.max)

        def hits(t):
            nc.vector.tensor_tensor(window[t][:, V:], alf_pairs[t][:, 0, :], alf_pairs[t][:, 1, :], ALU.max)

        def weighted(t, h):
            nc.vector.tensor_tensor(by_lines(wf[t][:, h]), ft[t][h], by_lines(we[t][:, :, rays[h]]), ALU.mult)

        def ray_sums_on_tensor(t):
            turned = psum.tile([P, HALVES, P], F32, name="turned", bufs=1)
            for h in range(HALVES):
                for d in range(D):
                    nc.tensor.matmul(turned[:, h, :], wf[t][:, h, d, :], ident[:], is_transpose=True, start=(d == 0), stop=(d == D - 1))
            turned_sb = ring.tile([P, HALVES, P], F32, name="turned_sb")
            nc.scalar.copy(turned_sb[:], turned[:])
            ray[t] = psum.tile([P, V], F32, name="ray_bank", bufs=1)
            for h in range(HALVES):
                nc.tensor.transpose(ray[t][:, rays[h]], turned_sb[:, h, :], ident[:])

        def shade(t, sums, vs):
            nc.vector.scalar_tensor_tensor(window[t][:, vs], sums, gain[:, t : t + 1], window[t][:, shifted(vs, V)], ALU.mult, ALU.mult)

        def by_pixel(t, first, count):
            return window[t][:].indirect(pix_sb[:, first // 16 : (first + count) // 16])

        def look_up(t):
            for h in range(2):
                nc.scalar.activation(picked[h][:, t, :], by_pixel(t, h * PIX_HALF, PIX_HALF), ACT.Copy)
            if t == 1:
                for h in range(2):
                    nc.scalar.copy(woven[h][:, :, 0:2], picked[h][:, 0:2, :].rearrange("p t r -> p r t"))

        for t in range(PACK):
            far = sigmoids(t)
            if t == 0:
                for h in range(HALVES):
                    nc.vector.tensor_scalar(recip[t][:, :, rays[h]], far[:, :, rays[h]], -10.0 * RATIO, -RATIO, ALU.mult, ALU.add)
                    if h == 1:
                        opacities(t, rays[0])
                    ratios(t, rays[h])
                weights_inside(t, rays[0])
                opacities(t, rays[1])
                largest_of_pairs_in(t, rays[0])
                weights_inside(t, rays[1])
                largest_of_pairs_in(t, rays[1])
            else:
                ratios(t, every_ray)
                if t >= 2:
                    shade(t - 2, ray[t - 2][:], every_ray)
                    look_up(t - 2)
                weighted(t - 1, 0)
                opacities(t, every_ray)
                weighted(t - 1, 1)
                ray_sums_on_tensor(t - 1)
                weights_inside(t, every_ray)
                if t < last:
                    largest_of_pairs_in(t, every_ray)
            weights_first(t)
            if t < last:
                hits(t)
        largest_of_pairs_in(last, every_ray)
        weighted(last, 0)
        shade(last - 1, ray[last - 1][:], every_ray)
        look_up(last - 1)
        weighted(last, 1)
        wf_pairs = keep.tile([P, HALVES, 2, P], F32, name="wf_pairs")
        ray_last = keep.tile([P, V], F32, name="ray_last")
        for h in range(HALVES):
            nc.vector.tensor_tensor(wf_pairs[:, h], wf[last][:, h, 0:2, :], wf[last][:, h, 2:4, :], ALU.add)
            if h == 0:
                hits(last)
        for h in range(HALVES):
            nc.vector.tensor_tensor(ray_last[:, rays[h]], wf_pairs[:, h, 0, :], wf_pairs[:, h, 1, :], ALU.add)
        for h in range(HALVES):
            shade(last, ray_last[:, rays[h]], rays[h])
        quarters = [slice(0, PIX_HALF // 2), slice(PIX_HALF // 2, PIX_HALF)]
        for rs in quarters:
            nc.vector.tensor_copy(picked[0][:, last, rs], by_pixel(last, rs.start, PIX_HALF // 2))
        nc.scalar.activation(picked[1][:, last, :], by_pixel(last, PIX_HALF, PIX_HALF), ACT.Copy)

        codes = [keep.tile([P, PIX_HALF], U32, name=f"codes{h}", align_bytes=64) for h in range(2)]
        planes = [keep.tile([P, PIX_HALF], U8, name=f"planes{h}", align_bytes=64) for h in range(2)]
        for rs in quarters:
            nc.vector.tensor_copy(woven[0][:, rs, 2:4], picked[0][:, 2:4, rs].rearrange("p t r -> p r t"))
        nc.scalar.copy(woven[1][:, :, 2:4], picked[1][:, 2:4, :].rearrange("p t r -> p r t"))
        for h in range(2):
            nc.vector.quantize_mx(out=codes[h][:].bitcast(FP8X4), scales=planes[h][:], in_=woven[h][:].rearrange("p r t -> p (r t)"))
            for m in range(N // P):
                acc = psum.tile([P, BANK], F32, name="sd", bufs=3)
                nc.tensor.matmul_mx(
                    out=acc[:, :PIX_HALF],
                    lhsT=ww_raw[:, 0, 2 * P * m : 2 * P * (m + 1)].bitcast(FP4X4),
                    lhsT_scale=ws_raw[0][:, 0, P * m : P * (m + 1)],
                    rhs=codes[h][:].bitcast(FP8X4),
                    rhs_scale=planes[h][:],
                    start=True,
                    stop=True,
                )
                result = keep.tile([P, PIX_HALF], F32, name=f"result{h}{m}")
                target = out[m * P : (m + 1) * P, h * PIX_HALF : (h + 1) * PIX_HALF]
                if h == 1 and m == 1:
                    nc.vector.tensor_copy(result[:], acc[:, :PIX_HALF])
                else:
                    nc.scalar.copy(result[:], acc[:, :PIX_HALF])
                nc.sync.dma_start(target, result[:])
